import numpy as np, ml_dtypes
CORES = [100,101,102,103,108,109,110,111]
N = 8
import mx_ref
NC = 512
BF = ml_dtypes.bfloat16
def setup_inputs(rng):
    def f(*shape):
        return mx_ref.flush((rng.standard_normal(shape, dtype=np.float32) * np.exp2(rng.integers(-2, 3, shape[:-1] + (1,)))).astype(BF))
    return {"c": f(N, 128, 512), "x": f(N, 128, 4 * NC)}
def setup_inputs_blocks(rng):
    d = setup_inputs(rng)
    for k in ("c", "x"): d[k] = mx_ref.spread(d[k], rng, 2)
    return d
def setup_inputs_wide(rng):
    d = setup_inputs(rng)
    for k in ("c", "x"): d[k] = mx_ref.flush((d[k].astype(np.float32) * np.exp2(rng.integers(-8, 9, (N, 1, 1))).astype(np.float32)).astype(BF))
    return d
def setup_inputs_zeros(rng):
    d = setup_inputs(rng); v = d["x"].reshape(N, 128, -1, 4).copy()
    v[np.broadcast_to((rng.random((N, 1, v.shape[2], 1)) < 0.33), v.shape)] = 0
    d["x"] = v.reshape(d["x"].shape)
    return d
def reference(c, x):
    QC = [mx_ref.quantize(c[k]) for k in range(N)]; QX = [mx_ref.quantize(x[j]) for j in range(N)]
    y = np.zeros((N, 128, NC), np.float32)
    for r in range(N):
        for j in range(N):
            p = mx_ref.matmul(QC[(r - j) % N], QX[j])
            y[r] = p if j == 0 else y[r] + p
    return {"y": y}

from concourse.bass import DstId, RemoteDMATransfer
from concourse.mybir import dt, ActivationFunctionType

N = 8
SIM_CORES = 112
CW = 128
XW = 512
SLOT = CW + XW
NCH = 2
XC = XW // NCH
BANK = 512
DIRECT_N = 3
DIRECT_P = 3

PIECES = {"c": ("qa", 0, CW), "s": ("sa", 0, SLOT)}
for _i in range(NCH):
    PIECES["x%d" % _i] = ("qa", CW + _i * XC, CW + (_i + 1) * XC)
LAST = "x%d" % (NCH - 1)
ORDER = ["c"] + ["x%d" % _i for _i in range(NCH - 1)] + ["s", LAST]

SCRATCH = {
    "cin": ("sbuf", [128, 4 * CW], "bfloat16"),
    "xin": ("sbuf", [128, 4 * XW], "bfloat16"),
    "qa": ("sbuf", [128, N * SLOT], "float8_e4m3fn_x4"),
    "sa": ("sbuf", [128, N * SLOT], "uint8"),
    "ps": ("psum", [128, NCH * BANK], "float32"),
    "yo": ("sbuf", [128, XW], "float32"),
}
SEMAPHORES = (["ldc", "qc", "sent"]
              + [n + str(i) for i in range(NCH) for n in ("ldx", "qx", "mm", "cp", "st")]
              + ["a%d%s" % (s, p) for s in range(N) for p in ORDER])


def _bits(mask):
    return [i for i in range(mask.bit_length()) if (mask >> i) & 1]


def _mask(bits):
    m = 0
    for b in bits:
        m |= 1 << b
    return m


def _groups(every, wide, n):
    share = 1
    while share * 2 * n <= len(every) and share * 2 <= len(wide):
        share *= 2
    out = wide[0::len(wide) // share]
    rest = [e for e in every if e not in out]
    return [out] + [rest[share * i:share * (i + 1)] for i in range(n - 1)]


def _plan(T, topo):
    cores = list(T.cores)
    chips = []
    for c in cores:
        if topo.chip(c) not in chips:
            chips.append(topo.chip(c))
    side = {ch: [c for c in cores if topo.chip(c) == ch] for ch in chips}
    jobs, taken = {}, []

    def helper(c, partner):
        h = [h for h in range(SIM_CORES)
             if topo.chip(h) == topo.chip(c) and topo.die(h) != topo.die(c) and h not in cores and h not in taken
             and (partner is None or topo.may_write(h, partner))][0]
        taken.append(h)
        return h

    info = {}
    for c in cores:
        here = side[topo.chip(c)]
        there = side[[ch for ch in chips if ch != topo.chip(c)][0]]
        info[c] = (there[here.index(c)], [m for m in here if m != c])
    relay = {c: helper(c, info[c][0]) for c in cores if not topo.may_write(c, info[c][0])}
    for c in cores:
        slot = T.rank_of(c)
        partner, mates = info[c]
        every = _bits(topo.mask(c, mates[0]))
        if c in relay:
            h = relay[c]
            near, far = mates[:DIRECT_N], mates[DIRECT_N:]
            link = _bits(topo.mask(h, partner))
            other = [e for e in _bits(topo.mask(h, c)) if e not in link]
            jobs[h] = [(slot, p, [(link, [partner])] + ([(other, far)] if far else [])) for p in ORDER]
            grp = _groups(every, every, 1 + len(near))
            copies = [(grp[0], [h])] + [(grp[1 + i], [m]) for i, m in enumerate(near)]
        else:
            near, far = mates[:DIRECT_P], mates[DIRECT_P:]
            grp = _groups(every, [e for e in every if e in _bits(topo.mask(c, partner))], 1 + len(near) + (1 if far else 0))
            copies = [(grp[0], [partner])] + [(grp[1 + i], [m]) for i, m in enumerate(near)]
            if far:
                h = helper(c, None)
                jobs[h] = [(slot, p, [(_bits(topo.mask(h, c)), far)]) for p in ORDER]
                copies.append((grp[-1], [h]))
        jobs[c] = ([(slot, p, copies) for p in ORDER]
                   + [(T.rank_of(partner), p, [(every, mates)]) for p in ORDER])
    arrive = {}
    for c in jobs:
        for slot, p, trs in jobs[c]:
            for eng, dsts in trs:
                for d in dsts:
                    arrive[(d, slot, p)] = len(eng)
    hops = {(c, T.rank_of(c)): 0 for c in cores}
    for _ in range(4):
        for c in jobs:
            for slot, p, trs in jobs[c]:
                if (c, slot) in hops:
                    for eng, dsts in trs:
                        for d in dsts:
                            hops[(d, slot)] = hops[(c, slot)] + 1
    return jobs, arrive, hops


def _view(T, slot, p):
    buf, a, b = PIECES[p]
    v = T[buf][:, slot * SLOT + a:slot * SLOT + b]
    return v.bitcast(dt.uint8) if buf == "qa" else v


def rank_program(g, core, T, topo):
    jobs, arrive, hops = _plan(T, topo)
    if core not in jobs:
        return
    rank = T.rank_of(core)
    sem = T.sem

    if rank is not None:
        base = rank * SLOT
        g.sync.dma_start(T.cin[:], T.c[:]).then_inc(sem.ldc, 16)
        for i in range(NCH):
            q = g.scalar if i % 2 == 0 else g.sync
            q.dma_start(T.xin[:, 4 * i * XC:4 * (i + 1) * XC], T.x[:, 4 * i * XC:4 * (i + 1) * XC]).then_inc(sem["ldx%d" % i], 16)
        g.vector.wait_ge(sem.ldc, 16)
        g.vector.quantize_mx(T.qa[:, base:base + CW], T.sa[:, base:base + CW], T.cin[:]).then_inc(sem.qc, 1)
        for i in range(NCH):
            a, b = base + CW + i * XC, base + CW + (i + 1) * XC
            g.vector.wait_ge(sem["ldx%d" % i], 16)
            g.vector.quantize_mx(T.qa[:, a:b], T.sa[:, a:b], T.xin[:, 4 * i * XC:4 * (i + 1) * XC]).then_inc(sem["qx%d" % i], 1)

    def ready(q, seen, slot, p):
        if slot == rank:
            name, val = {"c": "qc", "s": "qx%d" % (NCH - 1)}.get(p, "q" + p), 1
        else:
            name, val = "a%d%s" % (slot, p), arrive[(core, slot, p)]
        if name not in seen:
            seen.append(name)
            q.wait_ge(sem[name], val)

    sent, seen = 0, []
    for slot, p, trs in jobs[core]:
        ready(g, seen, slot, p)
        call = []
        for eng, dsts in trs:
            call.append(RemoteDMATransfer(
                dst_ids=[DstId(rid=topo.addr(d)[0], pnc=topo.addr(d)[1]) for d in dsts],
                dma_engine_mask=_mask(eng), remote_sem=sem["a%d%s" % (slot, p)],
                srcs=[_view(T, slot, p)], dsts=[_view(T, slot, p) for d in dsts]))
            sent += len(eng)
        g.remote_dma_fused(call, local_sem=sem.sent)
    g.wait_ge(sem.sent, sent)
    if rank is None:
        return

    todo = sorted((max(hops[(core, j)], hops[(core, (rank - j) % N)]), i, j) for j in range(N) for i in range(NCH))
    left, seen = [N] * NCH, []
    for _, i, j in todo:
        k = (rank - j) % N
        ready(g.tensor, seen, k, "c")
        if k != rank:
            ready(g.tensor, seen, k, "s")
        if j != rank:
            ready(g.tensor, seen, j, "s")
        ready(g.tensor, seen, j, "x%d" % i)
        w0, x0 = k * SLOT, j * SLOT + CW + i * XC
        mm = g.tensor.matmul_mx(T.ps[:, i * BANK:i * BANK + XC], T.qa[:, w0:w0 + CW], T.sa[:, w0:w0 + CW],
                                T.qa[:, x0:x0 + XC], T.sa[:, x0:x0 + XC], left[i] == N, left[i] == 1)
        left[i] -= 1
        if left[i] == 0:
            mm.then_inc(sem["mm%d" % i], 1)

    for i in range(NCH):
        out, bank = T.yo[:, i * XC:(i + 1) * XC], T.ps[:, i * BANK:i * BANK + XC]
        if i == NCH - 1:
            g.vector.wait_ge(sem["mm%d" % i], 1)
            g.vector.tensor_copy(out, bank).then_inc(sem["cp%d" % i], 1)
            q = g.sync
        else:
            g.scalar.wait_ge(sem["mm%d" % i], 1)
            g.scalar.activation(out, bank, ActivationFunctionType.Copy).then_inc(sem["cp%d" % i], 1)
            q = g.scalar
        q.wait_ge(sem["cp%d" % i], 1)
        q.dma_start(T.y[:, i * XC:(i + 1) * XC], out).then_inc(sem["st%d" % i], 16)
    for i in range(NCH):
        (g.sync if i == NCH - 1 else g.scalar).wait_ge(sem["st%d" % i], 16)
